import numpy as np
import ml_dtypes


def mxq(x, axis, fmt="e4m3"):
    dtype, down = {"e4m3": (ml_dtypes.float8_e4m3fn, 7), "e5m2": (ml_dtypes.float8_e5m2, 14)}[fmt]
    v = np.moveaxis(np.asarray(x, np.float32).astype(ml_dtypes.bfloat16).astype(np.float64), axis, -1)
    blocks = v.reshape(v.shape[:-1] + (-1, 32))
    amax = np.abs(blocks).max(-1, keepdims=True)
    byte = np.maximum(np.where(amax > 0, np.frexp(amax)[1] - 1 + 127, 0) - down, 1)
    scale = np.exp2(byte - 127.0)
    codes = (blocks / scale).astype(np.float32).astype(dtype).astype(np.float64)
    return np.moveaxis((codes * scale).reshape(v.shape), -1, axis)


WIDE = False


def mx_kscale(k):
    if not WIDE:
        return np.ones(k)
    levels = np.array([10, -10, 5, -5, 0])
    if k % 512:
        return np.exp2(np.random.permutation(np.resize(levels, k // 32))).repeat(32)
    a = np.empty((k // 512, 16))
    for p in range(k // 512):
        a[p, :8] = np.random.permutation(np.resize(levels, 8))
        for g in range(8):
            far = levels[np.abs(levels - a[p, g]) >= 10]
            a[p, g + 8] = far[np.random.randint(len(far))]
    return np.exp2(a.ravel()).repeat(32)


def f64(x):
    return np.asarray(x).astype(np.float64)


def striped(idx):
    return np.tile(np.asarray(idx).reshape(-1, 16).T, (8, 1)).astype(np.uint16)


def unstriped(offs):
    return offs[:16].T.reshape(-1).astype(np.int64)


B, N, T, D, DV, NQ = 1, 512, 2048, 512, 512, 256
CAP = 2.0


def setup_inputs():
    n = np.random.standard_normal
    idx = np.sort(np.random.permutation(T)[:B * N].reshape(B, N), axis=1).reshape(-1)
    s = mx_kscale(D)[:, None]
    u = np.ones(T)
    u[idx] = mx_kscale(B * N)
    r = np.random.uniform(0.5, 2.0, T)
    raw = n((D, T)) / s / (u * r)
    return {
        "qT": (n((B, D, NQ)) * s * (0.80 / np.sqrt(D))).astype(np.float32),
        "cT": raw.astype(np.float32),
        "ts": np.tile(u * r, (128, 1)).astype(np.float32),
        "ch": np.tile(s[:, 0] * np.random.uniform(0.5, 2.0, D), (128, 1)).astype(np.float32),
        "offs": striped(idx),
    }


def reference(qT, cT, ts, ch, offs):
    idx = unstriped(offs)
    c = f64(cT)
    pick = lambda x: x[:, idx].reshape(x.shape[0], B, N).transpose(1, 0, 2)
    q = f64(qT)
    score = mxq(q, 1, "e4m3").transpose(0, 2, 1) @ mxq(pick(c), 1, "e4m3")
    score = score * pick(f64(ts))[:, :1, :]
    score = CAP * np.tanh(score / CAP)
    m = score.max(-1, keepdims=True)
    p = np.exp(score - m)
    total = p.sum(-1, keepdims=True)
    w = p * pick(f64(ts))[:, :1, :]
    y = mxq(w, 2, "e4m3") @ mxq(pick(c).transpose(0, 2, 1), 1, "e4m3")
    y = y / total
    y = y * f64(ch)[:1]
    return y

@@ -1,0 +1,212 @@
+from contextlib import ExitStack
+
+import concourse.mybir as mybir
+from concourse.masks import make_identity
+
+F32 = mybir.dt.float32
+BF16 = mybir.dt.bfloat16
+U32 = mybir.dt.uint32
+U16 = mybir.dt.uint16
+U8 = mybir.dt.uint8
+FP8X4 = mybir.dt.float8_e4m3fn_x4
+ACT = mybir.ActivationFunctionType
+ALU = mybir.AluOpType
+AX = mybir.AxisListType
+
+P = 128
+PACK = 4
+TOKENS = 2048
+SLOTS = 512
+QUERIES = 256
+FEATURES = 512
+BLOCKS = QUERIES // P
+HALF = SLOTS // 2
+CAP = 2.0
+
+FLOPS = 2 * 2 * QUERIES * SLOTS * FEATURES
+
+
+def tile_attend_x_mla_cap_srt_kernel(tc, qT, cT, ts, ch, offs, out):
+    nc = tc.nc
+    with ExitStack() as ctx:
+        keep = ctx.enter_context(tc.tile_pool(name="keep", bufs=1))
+        psum_t = ctx.enter_context(tc.psum_pool(name="psum_t", bufs=2))
+        psum = ctx.enter_context(tc.psum_pool(name="psum", bufs=1))
+
+        offsets = keep.tile([P, SLOTS // 16], U16, name="offsets")
+        nc.sync.dma_start(offsets[:], offs)
+
+        plane_rows = cT.rearrange("(p j) w -> j p w", j=PACK)
+        first = keep.tile([P, TOKENS], F32, name="first")
+        nc.sync.dma_start(first[:], plane_rows[0])
+        q_raw = keep.tile([P, PACK, QUERIES], F32, name="q_raw")
+        nc.sync.dma_start(q_raw[:], qT[0].rearrange("(p j) q -> p j q", j=PACK))
+        rest = keep.tile([P, PACK - 1, TOKENS], F32, name="rest")
+        channel = keep.tile([P, FEATURES], F32, name="channel")
+        ts_row = keep.tile([P, TOKENS], F32, name="ts_row")
+        nc.vector.memset(ts_row[:], 0.0)
+        nc.sync.dma_start(ts_row[0:1, :], ts[0:1, :])
+        nc.vector.memset(rest[:, :, 0:1], 0.0)
+        nc.vector.memset(channel[:, 0:1], 0.0)
+        for t in range(PACK - 1):
+            nc.sync.dma_start(rest[:, t, :], plane_rows[t + 1])
+        nc.sync.dma_start(channel[:], ch)
+        planes = [first[:]] + [rest[:, t, :] for t in range(PACK - 1)]
+
+        ident32 = keep.tile([P, P], F32, name="ident32")
+        make_identity(nc, ident32[:])
+        ident16 = keep.tile([P, P], BF16, name="ident16")
+        make_identity(nc, ident16[:])
+        warm = keep.tile([P, 1], F32, name="warm")
+        nc.vector.memset(warm[:], 0.0)
+        nc.scalar.activation(warm[:], warm[:], ACT.Exp)
+
+        k_quads = keep.tile([P, SLOTS, PACK], BF16, name="k_quads", align_bytes=64)
+        k_codes = keep.tile([P, SLOTS], U32, name="k_codes", align_bytes=64)
+        k_scales = keep.tile([P, SLOTS], U8, name="k_scales", align_bytes=64)
+        v_quads = keep.tile([P, FEATURES, PACK], BF16, name="v_quads", align_bytes=64)
+        v_codes = keep.tile([P, FEATURES], U32, name="v_codes", align_bytes=64)
+        v_scales = keep.tile([P, FEATURES], U8, name="v_scales", align_bytes=64)
+        q_quads = keep.tile([P, QUERIES, PACK], BF16, name="q_quads", align_bytes=64)
+        q_codes = keep.tile([P, QUERIES], U32, name="q_codes", align_bytes=64)
+        q_scales = keep.tile([P, QUERIES], U8, name="q_scales", align_bytes=64)
+        w_quads = keep.tile([P, QUERIES, PACK], BF16, name="w_quads", align_bytes=64)
+        w_codes = keep.tile([P, QUERIES], U32, name="w_codes", align_bytes=64)
+        w_scales = keep.tile([P, QUERIES], U8, name="w_scales", align_bytes=64)
+
+        def quantize(codes, scales, quads, lo, hi):
+            nc.vector.quantize_mx(
+                out=codes[:, lo:hi].bitcast(FP8X4),
+                scales=scales[:, lo:hi],
+                in_=quads[:, lo:hi, :].rearrange("p n j -> p (n j)"),
+            )
+
+        by_place = k_quads[:].rearrange("p (s i) t -> p t i s", i=PACK)
+
+        def turn_plane(t):
+            turned = psum_t.tile([P, PACK, P], BF16, name="turned")
+            for i in range(PACK):
+                nc.tensor.transpose(turned[:, i, :], by_place[:, t, i, :], ident16[:])
+            nc.scalar.copy(v_quads[:, t * P : (t + 1) * P, :], turned[:].rearrange("s i p -> s p i"))
+
+        def gather_plane(t):
+            nc.vector.tensor_copy(k_quads[:, :, t], planes[t].indirect(offsets[:]))
+
+        gather_plane(0)
+        for b in range(BLOCKS):
+            rows = slice(b * P, (b + 1) * P)
+            nc.scalar.copy(q_quads[:, rows, :], q_raw[:, :, rows].rearrange("p j q -> p q j"))
+        turn_plane(0)
+        ts_slots = keep.tile([P, SLOTS], F32, name="ts_slots")
+        nc.vector.tensor_copy(ts_slots[:], ts_row[:].indirect(offsets[:]))
+        gather_plane(1)
+        quantize(q_codes, q_scales, q_quads, 0, QUERIES)
+        turn_plane(1)
+
+        ts_turned = psum_t.tile([P, PACK, P], F32, name="ts_turned", tag="turned")
+        for i in range(PACK):
+            nc.tensor.transpose(ts_turned[:, i, :], ts_slots[:, i * P : (i + 1) * P], ident32[:])
+        ts_column = keep.tile([P, PACK], F32, name="ts_column")
+        nc.scalar.copy(ts_column[:], ts_turned[:, :, 0])
+        ts_spread = psum_t.tile([P, SLOTS], F32, name="ts_spread", tag="turned")
+        for i in range(PACK):
+            nc.tensor.transpose(ts_spread[:, i * P : (i + 1) * P], ts_column[:, i : i + 1].to_broadcast([P, P]), ident32[:])
+        ts_all = keep.tile([P, SLOTS], F32, name="ts_all")
+        nc.scalar.copy(ts_all[:], ts_spread[:])
+
+        gather_plane(2)
+        turn_plane(2)
+
+        scores, scaled, capped, top, minus_m, weight, total = [], [], [], [], [], [], []
+        for b in range(BLOCKS):
+            scores.append(psum.tile([P, SLOTS], F32, name=f"scores{b}"))
+            scaled.append(keep.tile([P, SLOTS], F32, name=f"scaled{b}"))
+            capped.append(keep.tile([P, SLOTS], F32, name=f"capped{b}"))
+            top.append(keep.tile([P, 1], F32, name=f"top{b}"))
+            minus_m.append(keep.tile([P, 1], F32, name=f"minus_m{b}"))
+            total.append(keep.tile([P, 1], F32, name=f"total{b}"))
+            weight.append(keep.tile([P, SLOTS], BF16, name=f"weight{b}"))
+
+        def gather_last(h):
+            nc.vector.tensor_copy(
+                k_quads[:, h * HALF : (h + 1) * HALF, 3],
+                planes[3].indirect(offsets[:, h * HALF // 16 : (h + 1) * HALF // 16]),
+            )
+
+        def multiply_scores(h):
+            cols = slice(h * HALF, (h + 1) * HALF)
+            for b in range(BLOCKS):
+                rows = slice(b * P, (b + 1) * P)
+                nc.tensor.matmul_mx(
+                    out=scores[b][:, cols],
+                    lhsT=q_codes[:, rows].bitcast(FP8X4),
+                    lhsT_scale=q_scales[:, rows],
+                    rhs=k_codes[:, cols].bitcast(FP8X4),
+                    rhs_scale=k_scales[:, cols],
+                    start=True,
+                    stop=True,
+                )
+
+        def cap_scores(h):
+            cols = slice(h * HALF, (h + 1) * HALF)
+            for b in range(BLOCKS):
+                nc.vector.tensor_tensor(scaled[b][:, cols], scores[b][:, cols], ts_all[:, cols], ALU.mult)
+                nc.scalar.activation(capped[b][:, cols], scaled[b][:, cols], ACT.Tanh, scale=1.0 / CAP)
+
+        gather_last(0)
+        gather_last(1)
+        quantize(k_codes, k_scales, k_quads, 0, HALF)
+        multiply_scores(0)
+        quantize(k_codes, k_scales, k_quads, HALF, SLOTS)
+        multiply_scores(1)
+        quantize(v_codes, v_scales, v_quads, 0, 2 * P)
+        cap_scores(0)
+        cap_scores(1)
+        turn_plane(3)
+        for b in range(BLOCKS):
+            nc.vector.tensor_reduce(top[b][:], scaled[b][:], AX.X, ALU.max)
+            pair = keep.tile([P, 2], F32, name=f"pair{b}")
+            nc.scalar.activation(
+                pair[:], top[b][:].to_broadcast([P, 2]), ACT.Tanh, scale=-1.0 / CAP, accum_out=minus_m[b][:]
+            )
+        quantize(v_codes, v_scales, v_quads, 2 * P, 4 * P)
+        for b in range(BLOCKS):
+            rows = slice(b * P, (b + 1) * P)
+            prob = keep.tile([P, SLOTS], F32, name=f"prob{b}")
+            nc.scalar.activation(
+                prob[:], capped[b][:], ACT.Exp, bias=minus_m[b][:], scale=CAP, accum_out=total[b][:]
+            )
+            nc.vector.tensor_tensor(weight[b][:], prob[:], ts_all[:], ALU.mult)
+            words = weight[b][:].bitcast(F32)
+            w_turned = psum.tile([P, 2, P], F32, name=f"w_turned{b}")
+            for u in range(2):
+                nc.tensor.transpose(w_turned[:, u, :], words[:, u : SLOTS // 2 : 2], ident32[:])
+            nc.scalar.copy(
+                w_quads[:, rows, :].rearrange("p q j -> p (q j)").bitcast(F32).rearrange("p (q u) -> p q u", u=2),
+                w_turned[:].rearrange("p u q -> p q u"),
+            )
+        for b in range(BLOCKS):
+            rows = slice(b * P, (b + 1) * P)
+            quantize(w_codes, w_scales, w_quads, b * P, (b + 1) * P)
+            y = psum.tile([P, FEATURES], F32, name=f"y{b}")
+            nc.tensor.matmul_mx(
+                out=y[:],
+                lhsT=w_codes[:, rows].bitcast(FP8X4),
+                lhsT_scale=w_scales[:, rows],
+                rhs=v_codes[:].bitcast(FP8X4),
+                rhs_scale=v_scales[:],
+                start=True,
+                stop=True,
+            )
+            inverse = keep.tile([P, 1], F32, name=f"inverse{b}")
+            nc.vector.reciprocal(inverse[:], total[b][:])
+            result = keep.tile([P, FEATURES], F32, name=f"result{b}")
+            nc.vector.scalar_tensor_tensor(
+                result[:].rearrange("q (p t) -> q p t", t=PACK),
+                y[:].rearrange("q (t p) -> q p t", t=PACK),
+                inverse[:],
+                channel[:].rearrange("q (p t) -> q p t", t=PACK),
+                ALU.mult,
+                ALU.mult,
+            )
+            nc.sync.dma_start(out[0, rows, :], result[:])

@@ -39,17 +39,18 @@ def tile_attend_x_mla_cap_srt_kernel(tc, qT, cT, ts, ch, offs, out):
         plane_rows = cT.rearrange("(p j) w -> j p w", j=PACK)
         first = keep.tile([P, TOKENS], F32, name="first")
         nc.sync.dma_start(first[:], plane_rows[0])
-        q_raw = keep.tile([P, PACK, QUERIES], F32, name="q_raw")
-        nc.sync.dma_start(q_raw[:], qT[0].rearrange("(p j) q -> p j q", j=PACK))
-        rest = keep.tile([P, PACK - 1, TOKENS], F32, name="rest")
-        channel = keep.tile([P, FEATURES], F32, name="channel")
         ts_row = keep.tile([P, TOKENS], F32, name="ts_row")
         nc.vector.memset(ts_row[:], 0.0)
-        nc.sync.dma_start(ts_row[0:1, :], ts[0:1, :])
+        nc.scalar.dma_start(ts_row[0:1, :], ts[0:1, :])
+        rest = keep.tile([P, PACK - 1, TOKENS], F32, name="rest")
+        q_raw = keep.tile([P, PACK, QUERIES], F32, name="q_raw")
+        channel = keep.tile([P, FEATURES], F32, name="channel")
         nc.vector.memset(rest[:, :, 0:1], 0.0)
+        nc.vector.memset(q_raw[:, :, 0:1], 0.0)
         nc.vector.memset(channel[:, 0:1], 0.0)
         for t in range(PACK - 1):
             nc.sync.dma_start(rest[:, t, :], plane_rows[t + 1])
+        nc.sync.dma_start(q_raw[:], qT[0].rearrange("(p j) q -> p j q", j=PACK))
         nc.sync.dma_start(channel[:], ch)
         planes = [first[:]] + [rest[:, t, :] for t in range(PACK - 1)]
 
@@ -83,29 +84,22 @@ def tile_attend_x_mla_cap_srt_kernel(tc, qT, cT, ts, ch, offs, out):
 
         by_place = k_quads[:].rearrange("p (s i) t -> p t i s", i=PACK)
 
-        def turn_plane(t):
+        def turn_plane(t, copy):
             turned = psum_t.tile([P, PACK, P], BF16, name="turned")
             for i in range(PACK):
                 nc.tensor.transpose(turned[:, i, :], by_place[:, t, i, :], ident16[:])
-            nc.scalar.copy(v_quads[:, t * P : (t + 1) * P, :], turned[:].rearrange("s i p -> s p i"))
+            copy(v_quads[:, t * P : (t + 1) * P, :], turned[:].rearrange("s i p -> s p i"))
 
         def gather_plane(t):
             nc.vector.tensor_copy(k_quads[:, :, t], planes[t].indirect(offsets[:]))
 
         gather_plane(0)
-        for b in range(BLOCKS):
-            rows = slice(b * P, (b + 1) * P)
-            nc.scalar.copy(q_quads[:, rows, :], q_raw[:, :, rows].rearrange("p j q -> p q j"))
-        turn_plane(0)
+        turn_plane(0, nc.scalar.copy)
         ts_slots = keep.tile([P, SLOTS], F32, name="ts_slots")
         nc.vector.tensor_copy(ts_slots[:], ts_row[:].indirect(offsets[:]))
-        gather_plane(1)
-        quantize(q_codes, q_scales, q_quads, 0, QUERIES)
-        turn_plane(1)
-
         ts_turned = psum_t.tile([P, PACK, P], F32, name="ts_turned", tag="turned")
         for i in range(PACK):
-            nc.tensor.transpose(ts_turned[:, i, :], ts_slots[:, i * P : (i + 1) * P], ident32[:])
+            nc.tensor.transpose(ts_turned[:, i, :], ts_slots[:, i:SLOTS:PACK], ident32[:])
         ts_column = keep.tile([P, PACK], F32, name="ts_column")
         nc.scalar.copy(ts_column[:], ts_turned[:, :, 0])
         ts_spread = psum_t.tile([P, SLOTS], F32, name="ts_spread", tag="turned")
@@ -114,18 +108,10 @@ def tile_attend_x_mla_cap_srt_kernel(tc, qT, cT, ts, ch, offs, out):
         ts_all = keep.tile([P, SLOTS], F32, name="ts_all")
         nc.scalar.copy(ts_all[:], ts_spread[:])
 
+        gather_plane(1)
+        turn_plane(1, nc.scalar.copy)
         gather_plane(2)
-        turn_plane(2)
-
-        scores, scaled, capped, top, minus_m, weight, total = [], [], [], [], [], [], []
-        for b in range(BLOCKS):
-            scores.append(psum.tile([P, SLOTS], F32, name=f"scores{b}"))
-            scaled.append(keep.tile([P, SLOTS], F32, name=f"scaled{b}"))
-            capped.append(keep.tile([P, SLOTS], F32, name=f"capped{b}"))
-            top.append(keep.tile([P, 1], F32, name=f"top{b}"))
-            minus_m.append(keep.tile([P, 1], F32, name=f"minus_m{b}"))
-            total.append(keep.tile([P, 1], F32, name=f"total{b}"))
-            weight.append(keep.tile([P, SLOTS], BF16, name=f"weight{b}"))
+        quantize(v_codes, v_scales, v_quads, 0, 2 * P)
 
         def gather_last(h):
             nc.vector.tensor_copy(
@@ -133,64 +119,75 @@ def tile_attend_x_mla_cap_srt_kernel(tc, qT, cT, ts, ch, offs, out):
                 planes[3].indirect(offsets[:, h * HALF // 16 : (h + 1) * HALF // 16]),
             )
 
-        def multiply_scores(h):
-            cols = slice(h * HALF, (h + 1) * HALF)
-            for b in range(BLOCKS):
-                rows = slice(b * P, (b + 1) * P)
-                nc.tensor.matmul_mx(
-                    out=scores[b][:, cols],
-                    lhsT=q_codes[:, rows].bitcast(FP8X4),
-                    lhsT_scale=q_scales[:, rows],
-                    rhs=k_codes[:, cols].bitcast(FP8X4),
-                    rhs_scale=k_scales[:, cols],
-                    start=True,
-                    stop=True,
-                )
-
-        def cap_scores(h):
-            cols = slice(h * HALF, (h + 1) * HALF)
-            for b in range(BLOCKS):
-                nc.vector.tensor_tensor(scaled[b][:, cols], scores[b][:, cols], ts_all[:, cols], ALU.mult)
-                nc.scalar.activation(capped[b][:, cols], scaled[b][:, cols], ACT.Tanh, scale=1.0 / CAP)
-
         gather_last(0)
         gather_last(1)
-        quantize(k_codes, k_scales, k_quads, 0, HALF)
-        multiply_scores(0)
-        quantize(k_codes, k_scales, k_quads, HALF, SLOTS)
-        multiply_scores(1)
-        quantize(v_codes, v_scales, v_quads, 0, 2 * P)
-        cap_scores(0)
-        cap_scores(1)
-        turn_plane(3)
         for b in range(BLOCKS):
-            nc.vector.tensor_reduce(top[b][:], scaled[b][:], AX.X, ALU.max)
+            rows = slice(b * P, (b + 1) * P)
+            nc.scalar.copy(q_quads[:, rows, :], q_raw[:, :, rows].rearrange("p j q -> p q j"))
+        turn_plane(2, nc.scalar.copy)
+        scores, total, prob = [], [], []
+        for b in range(BLOCKS):
+            scores.append(psum.tile([P, SLOTS], F32, name=f"scores{b}"))
+            total.append(keep.tile([P, 1], F32, name=f"total{b}"))
+            prob.append(keep.tile([P, PACK, P], F32, name=f"prob{b}"))
+        for h in range(2):
+            quantize(k_codes, k_scales, k_quads, h * HALF, (h + 1) * HALF)
+        for b in range(BLOCKS):
+            rows = slice(b * P, (b + 1) * P)
+            quantize(q_codes, q_scales, q_quads, b * P, (b + 1) * P)
+            nc.tensor.matmul_mx(
+                out=scores[b][:],
+                lhsT=q_codes[:, rows].bitcast(FP8X4),
+                lhsT_scale=q_scales[:, rows],
+                rhs=k_codes[:].bitcast(FP8X4),
+                rhs_scale=k_scales[:],
+                start=True,
+                stop=True,
+            )
+        scaled, capped, minus_m = [], [], []
+        for b in range(BLOCKS):
+            scaled.append(keep.tile([P, PACK, P], F32, name=f"scaled{b}"))
+            capped.append(keep.tile([P, PACK, P], F32, name=f"capped{b}"))
+            minus_m.append(keep.tile([P, 1], F32, name=f"minus_m{b}"))
+        for b in range(BLOCKS):
+            nc.vector.tensor_tensor(
+                scaled[b][:],
+                scores[b][:].rearrange("q (s i) -> q i s", i=PACK),
+                ts_all[:].rearrange("q (i s) -> q i s", i=PACK),
+                ALU.mult,
+            )
+            nc.scalar.activation(capped[b][:], scaled[b][:], ACT.Tanh, scale=1.0 / CAP)
+        for b in range(BLOCKS):
+            top = keep.tile([P, 1], F32, name=f"top{b}")
+            nc.vector.tensor_reduce(top[:], scaled[b][:].rearrange("q i s -> q (i s)"), AX.X, ALU.max)
             pair = keep.tile([P, 2], F32, name=f"pair{b}")
             nc.scalar.activation(
-                pair[:], top[b][:].to_broadcast([P, 2]), ACT.Tanh, scale=-1.0 / CAP, accum_out=minus_m[b][:]
+                pair[:], top[:].to_broadcast([P, 2]), ACT.Tanh, scale=-1.0 / CAP, accum_out=minus_m[b][:]
             )
-        quantize(v_codes, v_scales, v_quads, 2 * P, 4 * P)
-        for b in range(BLOCKS):
-            rows = slice(b * P, (b + 1) * P)
-            prob = keep.tile([P, SLOTS], F32, name=f"prob{b}")
             nc.scalar.activation(
-                prob[:], capped[b][:], ACT.Exp, bias=minus_m[b][:], scale=CAP, accum_out=total[b][:]
+                prob[b][:], capped[b][:], ACT.Exp, bias=minus_m[b][:], scale=CAP, accum_out=total[b][:]
             )
-            nc.vector.tensor_tensor(weight[b][:], prob[:], ts_all[:], ALU.mult)
-            words = weight[b][:].bitcast(F32)
-            w_turned = psum.tile([P, 2, P], F32, name=f"w_turned{b}")
-            for u in range(2):
-                nc.tensor.transpose(w_turned[:, u, :], words[:, u : SLOTS // 2 : 2], ident32[:])
-            nc.scalar.copy(
-                w_quads[:, rows, :].rearrange("p q j -> p (q j)").bitcast(F32).rearrange("p (q u) -> p q u", u=2),
-                w_turned[:].rearrange("p u q -> p q u"),
-            )
+        turn_plane(3, nc.vector.tensor_copy)
+        turned_prob = []
+        for b in range(BLOCKS):
+            turned_prob.append(psum.tile([P, PACK, P], F32, name=f"turned_prob{b}"))
+            for i in range(PACK):
+                nc.tensor.transpose(turned_prob[b][:, i, :], prob[b][:, i, :], ident32[:])
+        y = []
         for b in range(BLOCKS):
             rows = slice(b * P, (b + 1) * P)
+            nc.vector.tensor_tensor(
+                w_quads[:, rows, :],
+                turned_prob[b][:].rearrange("s i q -> s q i"),
+                ts_column[:].unsqueeze(1).to_broadcast([P, P, PACK]),
+                ALU.mult,
+            )
+            if b == 0:
+                quantize(v_codes, v_scales, v_quads, 2 * P, 4 * P)
             quantize(w_codes, w_scales, w_quads, b * P, (b + 1) * P)
-            y = psum.tile([P, FEATURES], F32, name=f"y{b}")
+            y.append(psum.tile([P, FEATURES], F32, name=f"y{b}"))
             nc.tensor.matmul_mx(
-                out=y[:],
+                out=y[b][:],
                 lhsT=w_codes[:, rows].bitcast(FP8X4),
                 lhsT_scale=w_scales[:, rows],
                 rhs=v_codes[:].bitcast(FP8X4),
@@ -198,15 +195,20 @@ def tile_attend_x_mla_cap_srt_kernel(tc, qT, cT, ts, ch, offs, out):
                 start=True,
                 stop=True,
             )
+        for b in range(BLOCKS):
+            rows = slice(b * P, (b + 1) * P)
             inverse = keep.tile([P, 1], F32, name=f"inverse{b}")
             nc.vector.reciprocal(inverse[:], total[b][:])
-            result = keep.tile([P, FEATURES], F32, name=f"result{b}")
-            nc.vector.scalar_tensor_tensor(
-                result[:].rearrange("q (p t) -> q p t", t=PACK),
-                y[:].rearrange("q (t p) -> q p t", t=PACK),
-                inverse[:],
-                channel[:].rearrange("q (p t) -> q p t", t=PACK),
-                ALU.mult,
-                ALU.mult,
-            )
-            nc.sync.dma_start(out[0, rows, :], result[:])
+            result = keep.tile([P, P, PACK], F32, name=f"result{b}")
+            pieces = 1 if b == 0 else 2
+            for piece in range(pieces):
+                part = slice(piece * P // pieces, (piece + 1) * P // pieces)
+                nc.vector.scalar_tensor_tensor(
+                    result[:, part, :],
+                    y[b][:].rearrange("q (t p) -> q p t", t=PACK)[:, part, :],
+                    inverse[:],
+                    channel[:].rearrange("q (p t) -> q p t", t=PACK)[:, part, :],
+                    ALU.mult,
+                    ALU.mult,
+                )
+                nc.sync.dma_start(out[0, rows, :].rearrange("q (p t) -> q p t", t=PACK)[:, part, :], result[:, part, :])

@@ -37,22 +37,23 @@ def tile_attend_x_mla_cap_srt_kernel(tc, qT, cT, ts, ch, offs, out):
         nc.sync.dma_start(offsets[:], offs)
 
         plane_rows = cT.rearrange("(p j) w -> j p w", j=PACK)
-        first = keep.tile([P, TOKENS], F32, name="first")
-        nc.sync.dma_start(first[:], plane_rows[0])
+        early = keep.tile([P, 2, TOKENS], F32, name="early")
+        late = keep.tile([P, 2, TOKENS], F32, name="late")
+        planes = [early[:, 0, :], early[:, 1, :], late[:, 0, :], late[:, 1, :]]
+        for t in range(2):
+            nc.sync.dma_start(planes[t], plane_rows[t])
         ts_row = keep.tile([P, TOKENS], F32, name="ts_row")
         nc.vector.memset(ts_row[:], 0.0)
         nc.scalar.dma_start(ts_row[0:1, :], ts[0:1, :])
-        rest = keep.tile([P, PACK - 1, TOKENS], F32, name="rest")
         q_raw = keep.tile([P, PACK, QUERIES], F32, name="q_raw")
         channel = keep.tile([P, FEATURES], F32, name="channel")
-        nc.vector.memset(rest[:, :, 0:1], 0.0)
+        nc.vector.memset(late[:, :, 0:1], 0.0)
         nc.vector.memset(q_raw[:, :, 0:1], 0.0)
         nc.vector.memset(channel[:, 0:1], 0.0)
-        for t in range(PACK - 1):
-            nc.sync.dma_start(rest[:, t, :], plane_rows[t + 1])
+        for t in range(2, PACK):
+            nc.sync.dma_start(planes[t], plane_rows[t])
         nc.sync.dma_start(q_raw[:], qT[0].rearrange("(p j) q -> p j q", j=PACK))
         nc.sync.dma_start(channel[:], ch)
-        planes = [first[:]] + [rest[:, t, :] for t in range(PACK - 1)]
 
         ident32 = keep.tile([P, P], F32, name="ident32")
         make_identity(nc, ident32[:])
@@ -84,8 +85,7 @@ def tile_attend_x_mla_cap_srt_kernel(tc, qT, cT, ts, ch, offs, out):
 
         by_place = k_quads[:].rearrange("p (s i) t -> p t i s", i=PACK)
 
-        def turn_plane(t, copy):
-            turned = psum_t.tile([P, PACK, P], BF16, name="turned")
+        def turn_plane(t, copy, turned):
             for i in range(PACK):
                 nc.tensor.transpose(turned[:, i, :], by_place[:, t, i, :], ident16[:])
             copy(v_quads[:, t * P : (t + 1) * P, :], turned[:].rearrange("s i p -> s p i"))
@@ -94,7 +94,9 @@ def tile_attend_x_mla_cap_srt_kernel(tc, qT, cT, ts, ch, offs, out):
             nc.vector.tensor_copy(k_quads[:, :, t], planes[t].indirect(offsets[:]))
 
         gather_plane(0)
-        turn_plane(0, nc.scalar.copy)
+        turn_plane(0, nc.scalar.copy, psum_t.tile([P, PACK, P], BF16, name="turned"))
+        gather_plane(1)
+        turn_plane(1, nc.scalar.copy, psum_t.tile([P, PACK, P], BF16, name="turned"))
         ts_slots = keep.tile([P, SLOTS], F32, name="ts_slots")
         nc.vector.tensor_copy(ts_slots[:], ts_row[:].indirect(offsets[:]))
         ts_turned = psum_t.tile([P, PACK, P], F32, name="ts_turned", tag="turned")
@@ -108,10 +110,7 @@ def tile_attend_x_mla_cap_srt_kernel(tc, qT, cT, ts, ch, offs, out):
         ts_all = keep.tile([P, SLOTS], F32, name="ts_all")
         nc.scalar.copy(ts_all[:], ts_spread[:])
 
-        gather_plane(1)
-        turn_plane(1, nc.scalar.copy)
         gather_plane(2)
-        quantize(v_codes, v_scales, v_quads, 0, 2 * P)
 
         def gather_last(h):
             nc.vector.tensor_copy(
@@ -124,7 +123,6 @@ def tile_attend_x_mla_cap_srt_kernel(tc, qT, cT, ts, ch, offs, out):
         for b in range(BLOCKS):
             rows = slice(b * P, (b + 1) * P)
             nc.scalar.copy(q_quads[:, rows, :], q_raw[:, :, rows].rearrange("p j q -> p q j"))
-        turn_plane(2, nc.scalar.copy)
         scores, total, prob = [], [], []
         for b in range(BLOCKS):
             scores.append(psum.tile([P, SLOTS], F32, name=f"scores{b}"))
@@ -135,6 +133,8 @@ def tile_attend_x_mla_cap_srt_kernel(tc, qT, cT, ts, ch, offs, out):
         for b in range(BLOCKS):
             rows = slice(b * P, (b + 1) * P)
             quantize(q_codes, q_scales, q_quads, b * P, (b + 1) * P)
+            if b == 0:
+                quantize(v_codes, v_scales, v_quads, 0, 2 * P)
             nc.tensor.matmul_mx(
                 out=scores[b][:],
                 lhsT=q_codes[:, rows].bitcast(FP8X4),
@@ -167,23 +167,25 @@ def tile_attend_x_mla_cap_srt_kernel(tc, qT, cT, ts, ch, offs, out):
             nc.scalar.activation(
                 prob[b][:], capped[b][:], ACT.Exp, bias=minus_m[b][:], scale=CAP, accum_out=total[b][:]
             )
-        turn_plane(3, nc.vector.tensor_copy)
+        for t in range(2, PACK):
+            turn_plane(t, nc.vector.tensor_copy, psum.tile([P, PACK, P], BF16, name=f"turned{t}", tag=f"scores{t - 2}"))
         turned_prob = []
         for b in range(BLOCKS):
             turned_prob.append(psum.tile([P, PACK, P], F32, name=f"turned_prob{b}"))
             for i in range(PACK):
                 nc.tensor.transpose(turned_prob[b][:, i, :], prob[b][:, i, :], ident32[:])
-        y = []
+        quantize(v_codes, v_scales, v_quads, 2 * P, 3 * P)
         for b in range(BLOCKS):
-            rows = slice(b * P, (b + 1) * P)
             nc.vector.tensor_tensor(
-                w_quads[:, rows, :],
+                w_quads[:, b * P : (b + 1) * P, :],
                 turned_prob[b][:].rearrange("s i q -> s q i"),
                 ts_column[:].unsqueeze(1).to_broadcast([P, P, PACK]),
                 ALU.mult,
             )
-            if b == 0:
-                quantize(v_codes, v_scales, v_quads, 2 * P, 4 * P)
+        quantize(v_codes, v_scales, v_quads, 3 * P, 4 * P)
+        y = []
+        for b in range(BLOCKS):
+            rows = slice(b * P, (b + 1) * P)
             quantize(w_codes, w_scales, w_quads, b * P, (b + 1) * P)
             y.append(psum.tile([P, FEATURES], F32, name=f"y{b}"))
             nc.tensor.matmul_mx(

from contextlib import ExitStack

import concourse.mybir as mybir
from concourse.masks import make_identity

F32 = mybir.dt.float32
BF16 = mybir.dt.bfloat16
U32 = mybir.dt.uint32
U16 = mybir.dt.uint16
U8 = mybir.dt.uint8
FP8X4 = mybir.dt.float8_e4m3fn_x4
ACT = mybir.ActivationFunctionType
ALU = mybir.AluOpType
AX = mybir.AxisListType

P = 128
PACK = 4
TOKENS = 2048
SLOTS = 512
QUERIES = 256
FEATURES = 512
BLOCKS = QUERIES // P
HALF = SLOTS // 2
CAP = 2.0

FLOPS = 2 * 2 * QUERIES * SLOTS * FEATURES


def tile_attend_x_mla_cap_srt_kernel(tc, qT, cT, ts, ch, offs, out):
    nc = tc.nc
    with ExitStack() as ctx:
        keep = ctx.enter_context(tc.tile_pool(name="keep", bufs=1))
        psum_t = ctx.enter_context(tc.psum_pool(name="psum_t", bufs=2))
        psum = ctx.enter_context(tc.psum_pool(name="psum", bufs=1))

        offsets = keep.tile([P, SLOTS // 16], U16, name="offsets")
        nc.sync.dma_start(offsets[:], offs)

        plane_rows = cT.rearrange("(p j) w -> j p w", j=PACK)
        early = keep.tile([P, 2, TOKENS], F32, name="early")
        late = keep.tile([P, 2, TOKENS], F32, name="late")
        planes = [early[:, 0, :], early[:, 1, :], late[:, 0, :], late[:, 1, :]]
        for t in range(2):
            nc.sync.dma_start(planes[t], plane_rows[t])
        ts_row = keep.tile([P, TOKENS], F32, name="ts_row")
        nc.vector.memset(ts_row[:], 0.0)
        nc.scalar.dma_start(ts_row[0:1, :], ts[0:1, :])
        q_raw = keep.tile([P, PACK, QUERIES], F32, name="q_raw")
        channel = keep.tile([P, FEATURES], F32, name="channel")
        nc.vector.memset(late[:, :, 0:1], 0.0)
        nc.vector.memset(q_raw[:, :, 0:1], 0.0)
        nc.vector.memset(channel[:, 0:1], 0.0)
        for t in range(2, PACK):
            nc.sync.dma_start(planes[t], plane_rows[t])
        nc.sync.dma_start(q_raw[:], qT[0].rearrange("(p j) q -> p j q", j=PACK))
        nc.sync.dma_start(channel[:], ch)

        ident32 = keep.tile([P, P], F32, name="ident32")
        make_identity(nc, ident32[:])
        ident16 = keep.tile([P, P], BF16, name="ident16")
        make_identity(nc, ident16[:])
        warm = keep.tile([P, 1], F32, name="warm")
        nc.vector.memset(warm[:], 0.0)
        nc.scalar.activation(warm[:], warm[:], ACT.Exp)

        k_quads = keep.tile([P, SLOTS, PACK], BF16, name="k_quads", align_bytes=64)
        k_codes = keep.tile([P, SLOTS], U32, name="k_codes", align_bytes=64)
        k_scales = keep.tile([P, SLOTS], U8, name="k_scales", align_bytes=64)
        v_quads = keep.tile([P, FEATURES, PACK], BF16, name="v_quads", align_bytes=64)
        v_codes = keep.tile([P, FEATURES], U32, name="v_codes", align_bytes=64)
        v_scales = keep.tile([P, FEATURES], U8, name="v_scales", align_bytes=64)
        q_quads = keep.tile([P, QUERIES, PACK], BF16, name="q_quads", align_bytes=64)
        q_codes = keep.tile([P, QUERIES], U32, name="q_codes", align_bytes=64)
        q_scales = keep.tile([P, QUERIES], U8, name="q_scales", align_bytes=64)
        w_quads = keep.tile([P, QUERIES, PACK], BF16, name="w_quads", align_bytes=64)
        w_codes = keep.tile([P, QUERIES], U32, name="w_codes", align_bytes=64)
        w_scales = keep.tile([P, QUERIES], U8, name="w_scales", align_bytes=64)

        def quantize(codes, scales, quads, lo, hi):
            nc.vector.quantize_mx(
                out=codes[:, lo:hi].bitcast(FP8X4),
                scales=scales[:, lo:hi],
                in_=quads[:, lo:hi, :].rearrange("p n j -> p (n j)"),
            )

        by_place = k_quads[:].rearrange("p (s i) t -> p t i s", i=PACK)

        def turn_plane(t, copy, turned):
            for i in range(PACK):
                nc.tensor.transpose(turned[:, i, :], by_place[:, t, i, :], ident16[:])
            copy(v_quads[:, t * P : (t + 1) * P, :], turned[:].rearrange("s i p -> s p i"))

        def gather_plane(t):
            nc.vector.tensor_copy(k_quads[:, :, t], planes[t].indirect(offsets[:]))

        gather_plane(0)
        turn_plane(0, nc.scalar.copy, psum_t.tile([P, PACK, P], BF16, name="turned"))
        gather_plane(1)
        turn_plane(1, nc.scalar.copy, psum_t.tile([P, PACK, P], BF16, name="turned"))
        ts_slots = keep.tile([P, SLOTS], F32, name="ts_slots")
        nc.vector.tensor_copy(ts_slots[:], ts_row[:].indirect(offsets[:]))
        ts_turned = psum_t.tile([P, PACK, P], F32, name="ts_turned", tag="turned")
        for i in range(PACK):
            nc.tensor.transpose(ts_turned[:, i, :], ts_slots[:, i:SLOTS:PACK], ident32[:])
        ts_column = keep.tile([P, PACK], F32, name="ts_column")
        nc.scalar.copy(ts_column[:], ts_turned[:, :, 0])
        ts_spread = psum_t.tile([P, SLOTS], F32, name="ts_spread", tag="turned")
        for i in range(PACK):
            nc.tensor.transpose(ts_spread[:, i * P : (i + 1) * P], ts_column[:, i : i + 1].to_broadcast([P, P]), ident32[:])
        ts_all = keep.tile([P, SLOTS], F32, name="ts_all")
        nc.scalar.copy(ts_all[:], ts_spread[:])

        gather_plane(2)

        def gather_last(h):
            nc.vector.tensor_copy(
                k_quads[:, h * HALF : (h + 1) * HALF, 3],
                planes[3].indirect(offsets[:, h * HALF // 16 : (h + 1) * HALF // 16]),
            )

        gather_last(0)
        gather_last(1)
        for b in range(BLOCKS):
            rows = slice(b * P, (b + 1) * P)
            nc.scalar.copy(q_quads[:, rows, :], q_raw[:, :, rows].rearrange("p j q -> p q j"))
        scores, total, prob = [], [], []
        for b in range(BLOCKS):
            scores.append(psum.tile([P, SLOTS], F32, name=f"scores{b}"))
            total.append(keep.tile([P, 1], F32, name=f"total{b}"))
            prob.append(keep.tile([P, PACK, P], F32, name=f"prob{b}"))
        for h in range(2):
            quantize(k_codes, k_scales, k_quads, h * HALF, (h + 1) * HALF)
        for b in range(BLOCKS):
            rows = slice(b * P, (b + 1) * P)
            quantize(q_codes, q_scales, q_quads, b * P, (b + 1) * P)
            if b == 0:
                quantize(v_codes, v_scales, v_quads, 0, 2 * P)
            nc.tensor.matmul_mx(
                out=scores[b][:],
                lhsT=q_codes[:, rows].bitcast(FP8X4),
                lhsT_scale=q_scales[:, rows],
                rhs=k_codes[:].bitcast(FP8X4),
                rhs_scale=k_scales[:],
                start=True,
                stop=True,
            )
        scaled, capped, minus_m = [], [], []
        for b in range(BLOCKS):
            scaled.append(keep.tile([P, PACK, P], F32, name=f"scaled{b}"))
            capped.append(keep.tile([P, PACK, P], F32, name=f"capped{b}"))
            minus_m.append(keep.tile([P, 1], F32, name=f"minus_m{b}"))
        for b in range(BLOCKS):
            nc.vector.tensor_tensor(
                scaled[b][:],
                scores[b][:].rearrange("q (s i) -> q i s", i=PACK),
                ts_all[:].rearrange("q (i s) -> q i s", i=PACK),
                ALU.mult,
            )
            nc.scalar.activation(capped[b][:], scaled[b][:], ACT.Tanh, scale=1.0 / CAP)
        for b in range(BLOCKS):
            top = keep.tile([P, 1], F32, name=f"top{b}")
            nc.vector.tensor_reduce(top[:], scaled[b][:].rearrange("q i s -> q (i s)"), AX.X, ALU.max)
            pair = keep.tile([P, 2], F32, name=f"pair{b}")
            nc.scalar.activation(
                pair[:], top[:].to_broadcast([P, 2]), ACT.Tanh, scale=-1.0 / CAP, accum_out=minus_m[b][:]
            )
            nc.scalar.activation(
                prob[b][:], capped[b][:], ACT.Exp, bias=minus_m[b][:], scale=CAP, accum_out=total[b][:]
            )
        for t in range(2, PACK):
            turn_plane(t, nc.vector.tensor_copy, psum.tile([P, PACK, P], BF16, name=f"turned{t}", tag=f"scores{t - 2}"))
        turned_prob = []
        for b in range(BLOCKS):
            turned_prob.append(psum.tile([P, PACK, P], F32, name=f"turned_prob{b}"))
            for i in range(PACK):
                nc.tensor.transpose(turned_prob[b][:, i, :], prob[b][:, i, :], ident32[:])
        quantize(v_codes, v_scales, v_quads, 2 * P, 3 * P)
        for b in range(BLOCKS):
            nc.vector.tensor_tensor(
                w_quads[:, b * P : (b + 1) * P, :],
                turned_prob[b][:].rearrange("s i q -> s q i"),
                ts_column[:].unsqueeze(1).to_broadcast([P, P, PACK]),
                ALU.mult,
            )
        quantize(v_codes, v_scales, v_quads, 3 * P, 4 * P)
        y = []
        for b in range(BLOCKS):
            rows = slice(b * P, (b + 1) * P)
            quantize(w_codes, w_scales, w_quads, b * P, (b + 1) * P)
            y.append(psum.tile([P, FEATURES], F32, name=f"y{b}"))
            nc.tensor.matmul_mx(
                out=y[b][:],
                lhsT=w_codes[:, rows].bitcast(FP8X4),
                lhsT_scale=w_scales[:, rows],
                rhs=v_codes[:].bitcast(FP8X4),
                rhs_scale=v_scales[:],
                start=True,
                stop=True,
            )
        for b in range(BLOCKS):
            rows = slice(b * P, (b + 1) * P)
            inverse = keep.tile([P, 1], F32, name=f"inverse{b}")
            nc.vector.reciprocal(inverse[:], total[b][:])
            result = keep.tile([P, P, PACK], F32, name=f"result{b}")
            pieces = 1 if b == 0 else 2
            for piece in range(pieces):
                part = slice(piece * P // pieces, (piece + 1) * P // pieces)
                nc.vector.scalar_tensor_tensor(
                    result[:, part, :],
                    y[b][:].rearrange("q (t p) -> q p t", t=PACK)[:, part, :],
                    inverse[:],
                    channel[:].rearrange("q (p t) -> q p t", t=PACK)[:, part, :],
                    ALU.mult,
                    ALU.mult,
                )
                nc.sync.dma_start(out[0, rows, :].rearrange("q (p t) -> q p t", t=PACK)[:, part, :], result[:, part, :])
